import numpy as np
import ml_dtypes


def mxq(x, axis, fmt="e4m3"):
    dtype, down = {"e4m3": (ml_dtypes.float8_e4m3fn, 7), "e5m2": (ml_dtypes.float8_e5m2, 14)}[fmt]
    v = np.moveaxis(np.asarray(x, np.float32).astype(ml_dtypes.bfloat16).astype(np.float64), axis, -1)
    blocks = v.reshape(v.shape[:-1] + (-1, 32))
    amax = np.abs(blocks).max(-1, keepdims=True)
    byte = np.maximum(np.where(amax > 0, np.frexp(amax)[1] - 1 + 127, 0) - down, 1)
    scale = np.exp2(byte - 127.0)
    codes = (blocks / scale).astype(np.float32).astype(dtype).astype(np.float64)
    return np.moveaxis((codes * scale).reshape(v.shape), -1, axis)


WIDE = False


def mx_kscale(k, group=512):
    if not WIDE:
        return np.ones(k)
    levels = np.array([10, -10, 5, -5, 0])
    if group != 512:
        return np.exp2(np.random.permutation(np.resize(levels, k // group))).repeat(group)
    if k % 512:
        return np.exp2(np.random.permutation(np.resize(levels, k // 32))).repeat(32)
    a = np.empty((k // 512, 16))
    for p in range(k // 512):
        a[p, :8] = np.random.permutation(np.resize(levels, 8))
        for g in range(8):
            far = levels[np.abs(levels - a[p, g]) >= 10]
            a[p, g + 8] = far[np.random.randint(len(far))]
    return np.exp2(a.ravel()).repeat(32)


def f64(x):
    return np.asarray(x).astype(np.float64)


def striped(idx):
    return np.tile(np.asarray(idx).reshape(-1, 16).T, (8, 1)).astype(np.uint16)


def unstriped(offs):
    return offs[:16].T.reshape(-1).astype(np.int64)


H, KV, D, NQ, N = 4, 1, 128, 512, 512


def setup_inputs():
    n = np.random.standard_normal
    s = mx_kscale(D, 0)[:, None]
    u = mx_kscale(N)
    t = np.random.uniform(0.5, 2.0, N) * u
    v = n((KV, N, 128))
    return {
        "qT": (n((H, D, NQ)) * s * (0.70 / np.sqrt(D))).astype(np.float32),
        "kT": (n((KV, D, N)) / s).astype(np.float32),
        "t": t.reshape(N, 1).astype(np.float32),
        "v": (v / t[:, None]).astype(np.float32),
        "kb": (0.5 * n((N, 1))).astype(np.float32),
        "gn": np.tile(np.random.uniform(0.5, 2.0, 128), (128, 1)).astype(np.float32),
    }


def reference(qT, kT, t, v, kb, gn):
    a = np.repeat(mxq(f64(kT), 1, "e4m3"), H // KV, 0).transpose(0, 2, 1) @ mxq(f64(qT), 1, "e4m3")
    a = a + f64(kb)
    p = 1.0 / (1.0 + np.exp(-a))
    w = p * f64(t)
    y = mxq(w, 1, "e4m3").transpose(0, 2, 1) @ np.repeat(mxq(f64(v), 1, "e4m3"), H // KV, 0)
    y = y / 16.0
    y = y / np.sqrt(np.mean(np.square(y), -1, keepdims=True) + 1e-5) * f64(gn)[:1]
    return y

@@ -1,0 +1,239 @@
+from contextlib import ExitStack
+
+import concourse.mybir as mybir
+
+H, D, NQ, N, E = 4, 128, 512, 512, 128
+FLOPS = 2 * H * N * NQ * (D + E)
+
+F32 = mybir.dt.float32
+BF16 = mybir.dt.bfloat16
+U32 = mybir.dt.uint32
+U8 = mybir.dt.uint8
+FP8X4 = mybir.dt.float8_e4m3fn_x4
+ACT = mybir.ActivationFunctionType
+ALU = mybir.AluOpType
+
+P = 128
+PACK = 4
+ROWS = 32
+QC = 128
+CHUNKS = NQ // QC
+UNITS = CHUNKS * H
+HALF = N // 2
+S_HALF = HALF // PACK
+S_SPLIT = 40
+EPS = 256.0 * 1e-5
+BATCHES = ((0, 4), (4, 8), (8, 12), (12, 14), (14, 16))
+STORES = ((0, 2), (2, 4), (4, 6), (6, 8), (8, 10), (10, 12), (12, 14), (14, 15), (15, 16))
+
+
+def tile_rows_a_sigmoid_kb_onorm_kernel(tc, qT, kT, t, v, kb, gn, out):
+    nc = tc.nc
+    with ExitStack() as ctx:
+        keep = ctx.enter_context(tc.tile_pool(name="keep", bufs=1))
+        work = ctx.enter_context(tc.tile_pool(name="work", bufs=4))
+        psum = ctx.enter_context(tc.psum_pool(name="psum", bufs=1))
+        ctx.enter_context(tc.manual_schedule())
+
+        s_bank = [psum.tile([P, PACK, QC], F32, name="s_bank%d" % g) for g in range(H)]
+        y_bank = [psum.tile([P, PACK, E], F32, name="y_bank%d" % b) for b in range(4)]
+
+        q_raw = [keep.tile([P, PACK, QC], F32, name="q_raw%d" % c) for c in range(CHUNKS)]
+        q_bf = [keep.tile([P, QC, PACK], BF16, name="q_bf%d" % c, align_bytes=64) for c in range(CHUNKS)]
+        q_codes = [keep.tile([P, QC], U32, name="q_codes%d" % c, align_bytes=64) for c in range(CHUNKS)]
+        q_scales = [keep.tile([P, QC], U8, name="q_scales%d" % c, align_bytes=64) for c in range(CHUNKS)]
+        k_raw = [keep.tile([P, PACK, HALF], F32, name="k_raw%d" % a) for a in range(2)]
+        k_bf = keep.tile([P, PACK, P, PACK], BF16, align_bytes=64)
+        k_codes = keep.tile([P, N], U32, align_bytes=64)
+        k_scales = keep.tile([P, N], U8, align_bytes=64)
+        v_raw = keep.tile([P, PACK, E], F32)
+        v_bf = keep.tile([P, E, PACK], BF16, align_bytes=64)
+        v_codes = keep.tile([P, E], U32, align_bytes=64)
+        v_scales = keep.tile([P, E], U8, align_bytes=64)
+        t_sb = keep.tile([P, PACK], F32)
+        kb_sb = keep.tile([P, PACK], F32)
+        gn_sb = keep.tile([P, E], F32)
+        zero = keep.tile([P, 1], F32)
+        warm = keep.tile([P, 1], F32)
+        sumsq = keep.tile([P, UNITS], F32)
+        rstd = [keep.tile([P, hi - lo], F32, name="rstd%d" % lo) for lo, hi in BATCHES]
+        result = [keep.tile([P, hi - lo, E], F32, name="result%d" % lo) for lo, hi in STORES]
+
+        q_hbm = qT.rearrange("h (p j) q -> (h p) j q", j=PACK)
+        k_hbm = kT.rearrange("o (p j) i -> (o p) j i", j=PACK)
+
+        def load_q(c):
+            nc.sync.dma_start(out=q_raw[c][:], in_=q_hbm[:, :, QC * c : QC * (c + 1)])
+
+        nc.vector.memset(zero[:], 0.0)
+        load_q(0)
+        for a in range(2):
+            for g in (2, 0, 3, 1):
+                queue = nc.sync if g < 2 else nc.scalar
+                queue.dma_start(
+                    out=k_raw[a][ROWS * g : ROWS * (g + 1), :, :], in_=k_hbm[:, :, HALF * a : HALF * (a + 1)]
+                )
+        nc.scalar.activation(out=warm[:], in_=zero[:], func=ACT.Sigmoid)
+        nc.sync.dma_start(out=kb_sb[:], in_=kb.rearrange("(p r) o -> p (r o)", r=PACK))
+        nc.sync.dma_start(out=t_sb[:], in_=t.rearrange("(p r) o -> p (r o)", r=PACK))
+        load_q(1)
+        nc.sync.dma_start(out=v_raw[:], in_=v.rearrange("o (p r) e -> (o p) r e", r=PACK))
+        load_q(2)
+        nc.sync.dma_start(out=gn_sb[:], in_=gn)
+        load_q(3)
+
+        def interleave(dst, src):
+            nc.vector.tensor_copy(
+                out=dst[:].rearrange("p (a i) j -> p a j i", i=4), in_=src[:].rearrange("p j (a i) -> p a j i", i=4)
+            )
+
+        def quantize(codes, scales, src):
+            nc.vector.quantize_mx(out=codes.bitcast(FP8X4), scales=scales, in_=src)
+
+        def quantize_q(c):
+            quantize(q_codes[c][:], q_scales[c][:], q_bf[c][:].rearrange("p q j -> p (q j)"))
+
+        def deal_k(a, lo, hi):
+            dst = k_bf[:, :, S_HALF * a + lo : S_HALF * a + hi, :].rearrange("p r s j -> p s r j")
+            src = k_raw[a][:, :, PACK * lo : PACK * hi].rearrange("p j (s r) -> p s r j", r=PACK)
+            return dst, src
+
+        def quantize_k(r0):
+            cols = slice(P * r0, P * (r0 + 2))
+            quantize(k_codes[:, cols], k_scales[:, cols], k_bf[:, r0 : r0 + 2, :, :].rearrange("p r s j -> p (r s j)"))
+
+        def scores(*jobs):
+            for step in range(2):
+                for u, half in jobs:
+                    r = 2 * half + step
+                    c, g = divmod(u, H)
+                    rows = slice(ROWS * g, ROWS * (g + 1))
+                    cols = slice(P * r, P * (r + 1))
+                    nc.tensor.matmul_mx(
+                        out=s_bank[g][:, r, :],
+                        lhsT=k_codes[rows, cols].bitcast(FP8X4),
+                        lhsT_scale=k_scales[rows, cols],
+                        rhs=q_codes[c][rows, :].bitcast(FP8X4),
+                        rhs_scale=q_scales[c][rows, :],
+                        start=True,
+                        stop=True,
+                    )
+
+        prob, w_bf = {}, {}
+
+        def sigmoid(u):
+            prob[u] = work.tile([P, PACK, QC], F32, name="prob", bufs=UNITS)
+            for r in range(PACK):
+                nc.scalar.activation(
+                    out=prob[u][:, r, :], in_=s_bank[u % H][:, r, :], func=ACT.Sigmoid, bias=kb_sb[:, r : r + 1]
+                )
+
+        def weigh(u):
+            w_bf[u] = work.tile([P, QC, PACK], BF16, name="w_bf", align_bytes=64)
+            nc.vector.tensor_tensor(
+                out=w_bf[u][:].rearrange("p (a i) r -> p a r i", i=4),
+                in0=prob[u][:].rearrange("p r (a i) -> p a r i", i=4),
+                in1=t_sb[:].unsqueeze(1).unsqueeze(3).to_broadcast([P, QC // 4, PACK, 4]),
+                op=ALU.mult,
+            )
+
+        w_codes, w_scales = {}, {}
+
+        def quantize_w(u):
+            w_codes[u] = work.tile([P, QC], U32, name="w_codes", align_bytes=64, bufs=8)
+            w_scales[u] = work.tile([P, QC], U8, name="w_scales", align_bytes=64, bufs=8)
+            quantize(w_codes[u][:], w_scales[u][:], w_bf[u][:].rearrange("p q r -> p (q r)"))
+
+        def y_of(u):
+            return y_bank[(u // 2) % 4][:, 2 * (u // 8) + u % 2, :]
+
+        def values(u):
+            nc.tensor.matmul_mx(
+                out=y_of(u),
+                lhsT=w_codes[u][:].bitcast(FP8X4),
+                lhsT_scale=w_scales[u][:],
+                rhs=v_codes[:].bitcast(FP8X4),
+                rhs_scale=v_scales[:],
+                start=True,
+                stop=True,
+            )
+
+        def square(u):
+            squares = work.tile([P, E], BF16, name="squares")
+            nc.scalar.activation(out=squares[:], in_=y_of(u), func=ACT.Square, accum_out=sumsq[:, u : u + 1])
+
+        def root(b):
+            lo, hi = BATCHES[b]
+            nc.scalar.activation(
+                out=rstd[b][:], in_=sumsq[:, lo:hi], func=ACT.Abs_reciprocal_sqrt, scale=1.0 / E, bias=EPS
+            )
+
+        def finish(b):
+            lo, hi = BATCHES[b]
+            for u in range(lo, hi):
+                for i, (first, end) in enumerate(STORES):
+                    if first <= u < end:
+                        nc.vector.scalar_tensor_tensor(
+                            out=result[i][:, u - first, :],
+                            in0=y_of(u),
+                            scalar=rstd[b][:, u - lo : u - lo + 1],
+                            in1=gn_sb[:],
+                            op0=ALU.mult,
+                            op1=ALU.mult,
+                        )
+                    if u == end - 1:
+                        c, g = divmod(first, H)
+                        dst = out[g : g + end - first, QC * c : QC * (c + 1), :].rearrange("h q e -> q h e")
+                        nc.sync.dma_start(out=dst, in_=result[i][:])
+
+        interleave(q_bf[0], q_raw[0])
+        dst, src = deal_k(0, 0, S_HALF)
+        nc.vector.tensor_copy(out=dst, in_=src)
+        quantize_q(0)
+        dst, src = deal_k(1, 0, S_SPLIT)
+        nc.vector.tensor_copy(out=dst, in_=src)
+        dst, src = deal_k(1, S_SPLIT, S_HALF)
+        nc.scalar.copy(out=dst, in_=src)
+        quantize_k(0)
+        quantize_k(2)
+        scores((0, 0), (1, 0))
+        scores((0, 1), (1, 1))
+        scores((2, 0), (3, 0))
+        scores((2, 1))
+        interleave(q_bf[1], q_raw[1])
+        interleave(v_bf, v_raw)
+        quantize_q(1)
+        quantize(v_codes[:], v_scales[:], v_bf[:].rearrange("p e r -> p (e r)"))
+
+        for n in range(UNITS + 1):
+            if n < UNITS:
+                sigmoid(n)
+                if n + H < UNITS:
+                    scores((n + H - 1, 1), (n + H, 0))
+                elif n + H == UNITS:
+                    scores((n + H - 1, 1))
+                weigh(n)
+            if n >= 1:
+                quantize_w(n - 1)
+            if n in (0, 4):
+                interleave(q_bf[2 + n // 4], q_raw[2 + n // 4])
+            if n in (1, 5):
+                quantize_q(2 + n // 4)
+            if n in (5, 9):
+                for u in range(n - 5, n - 1):
+                    values(u)
+            if n == 12:
+                for u in range(8, 12):
+                    values(u)
+            if n > 12:
+                values(n - 1)
+
+        for b, (lo, hi) in enumerate(BATCHES):
+            for u in range(lo, hi):
+                square(u)
+                if u == lo and b >= 2:
+                    root(b - 1)
+                    finish(b - 1)
+            if b in (0, len(BATCHES) - 1):
+                root(b)
+                finish(b)

@@ -23,8 +23,18 @@ HALF = N // 2
 S_HALF = HALF // PACK
 S_SPLIT = 40
 EPS = 256.0 * 1e-5
-BATCHES = ((0, 4), (4, 8), (8, 12), (12, 14), (14, 16))
-STORES = ((0, 2), (2, 4), (4, 6), (6, 8), (8, 10), (10, 12), (12, 14), (14, 15), (15, 16))
+ALL = (0, 1, 2, 3)
+PLAN = (
+    (((0,), ALL), ((1,), ALL), ((2, 3), (0, 1)), ((2, 3), (2, 3))),
+    (((0,), ALL), ((1, 2), (0, 1)), ((1, 2), (2, 3)), ((3,), ALL)),
+    (((0,), ALL), ((1,), ALL), ((2, 3), (0, 1)), ((2, 3), (2, 3))),
+    (((0, 1), (0, 1)), ((0, 1), (2, 3)), ((2, 3), (0, 1)), ((2, 3), (2, 3))),
+)
+FILLS = tuple((n % H,) + PLAN[n % H][n // H] for n in range(UNITS))
+GROUPS = tuple((g, cs) for g, cs, rs in FILLS if rs[-1] == PACK - 1)
+UNIT = tuple((g, c) for g, cs in GROUPS for c in cs)
+BATCHES = ((0, 3), (3, 7), (7, 11), (11, 16))
+STORES = ((0, 3), (3, 4), (4, 5), (5, 7), (7, 9), (9, 11), (11, 12), (12, 14), (14, 15), (15, 16))
 
 
 def tile_rows_a_sigmoid_kb_onorm_kernel(tc, qT, kT, t, v, kb, gn, out):
@@ -35,7 +45,7 @@ def tile_rows_a_sigmoid_kb_onorm_kernel(tc, qT, kT, t, v, kb, gn, out):
         psum = ctx.enter_context(tc.psum_pool(name="psum", bufs=1))
         ctx.enter_context(tc.manual_schedule())
 
-        s_bank = [psum.tile([P, PACK, QC], F32, name="s_bank%d" % g) for g in range(H)]
+        s_bank = [psum.tile([P, PACK * QC], F32, name="s_bank%d" % g) for g in range(H)]
         y_bank = [psum.tile([P, PACK, E], F32, name="y_bank%d" % b) for b in range(4)]
 
         q_raw = [keep.tile([P, PACK, QC], F32, name="q_raw%d" % c) for c in range(CHUNKS)]
@@ -75,12 +85,12 @@ def tile_rows_a_sigmoid_kb_onorm_kernel(tc, qT, kT, t, v, kb, gn, out):
                 )
         nc.scalar.activation(out=warm[:], in_=zero[:], func=ACT.Sigmoid)
         nc.sync.dma_start(out=kb_sb[:], in_=kb.rearrange("(p r) o -> p (r o)", r=PACK))
-        nc.sync.dma_start(out=t_sb[:], in_=t.rearrange("(p r) o -> p (r o)", r=PACK))
         load_q(1)
-        nc.sync.dma_start(out=v_raw[:], in_=v.rearrange("o (p r) e -> (o p) r e", r=PACK))
+        nc.sync.dma_start(out=t_sb[:], in_=t.rearrange("(p r) o -> p (r o)", r=PACK))
         load_q(2)
-        nc.sync.dma_start(out=gn_sb[:], in_=gn)
         load_q(3)
+        nc.sync.dma_start(out=v_raw[:], in_=v.rearrange("o (p r) e -> (o p) r e", r=PACK))
+        nc.sync.dma_start(out=gn_sb[:], in_=gn)
 
         def interleave(dst, src):
             nc.vector.tensor_copy(
@@ -104,13 +114,14 @@ def tile_rows_a_sigmoid_kb_onorm_kernel(tc, qT, kT, t, v, kb, gn, out):
 
         def scores(*jobs):
             for step in range(2):
-                for u, half in jobs:
-                    r = 2 * half + step
-                    c, g = divmod(u, H)
+                for n, half in jobs:
+                    g, cs, rs = FILLS[n]
+                    place = 2 * half + step
+                    r, c = rs[place // len(cs)], cs[place % len(cs)]
                     rows = slice(ROWS * g, ROWS * (g + 1))
                     cols = slice(P * r, P * (r + 1))
                     nc.tensor.matmul_mx(
-                        out=s_bank[g][:, r, :],
+                        out=s_bank[g][:, QC * place : QC * (place + 1)],
                         lhsT=k_codes[rows, cols].bitcast(FP8X4),
                         lhsT_scale=k_scales[rows, cols],
                         rhs=q_codes[c][rows, :].bitcast(FP8X4),
@@ -119,39 +130,49 @@ def tile_rows_a_sigmoid_kb_onorm_kernel(tc, qT, kT, t, v, kb, gn, out):
                         stop=True,
                     )
 
-        prob, w_bf = {}, {}
+        prob = {}
+        for g, cs in GROUPS:
+            prob[g, cs] = keep.tile([P, PACK, QC * len(cs)], F32, name="prob%d_%d" % (g, cs[0]))
 
-        def sigmoid(u):
-            prob[u] = work.tile([P, PACK, QC], F32, name="prob", bufs=UNITS)
-            for r in range(PACK):
+        def sigmoid(n):
+            g, cs, rs = FILLS[n]
+            width = QC * len(cs)
+            for i, r in enumerate(rs):
                 nc.scalar.activation(
-                    out=prob[u][:, r, :], in_=s_bank[u % H][:, r, :], func=ACT.Sigmoid, bias=kb_sb[:, r : r + 1]
+                    out=prob[g, cs][:, r, :],
+                    in_=s_bank[g][:, width * i : width * (i + 1)],
+                    func=ACT.Sigmoid,
+                    bias=kb_sb[:, r : r + 1],
                 )
 
-        def weigh(u):
-            w_bf[u] = work.tile([P, QC, PACK], BF16, name="w_bf", align_bytes=64)
+        w_bf = keep.tile([P, UNITS * QC, PACK], BF16, align_bytes=64)
+        w_codes = keep.tile([P, UNITS * QC], U32, align_bytes=64)
+        w_scales = keep.tile([P, UNITS * QC], U8, align_bytes=64)
+
+        def weigh(first, end):
+            g, c = UNIT[first]
+            cs = [chunks for head, chunks in GROUPS if head == g and c in chunks][0]
+            lo = QC * cs.index(c)
+            width = QC * (end - first)
             nc.vector.tensor_tensor(
-                out=w_bf[u][:].rearrange("p (a i) r -> p a r i", i=4),
-                in0=prob[u][:].rearrange("p r (a i) -> p a r i", i=4),
-                in1=t_sb[:].unsqueeze(1).unsqueeze(3).to_broadcast([P, QC // 4, PACK, 4]),
+                out=w_bf[:, QC * first : QC * end, :].rearrange("p (a i) r -> p a r i", i=4),
+                in0=prob[g, cs][:, :, lo : lo + width].rearrange("p r (a i) -> p a r i", i=4),
+                in1=t_sb[:].unsqueeze(1).unsqueeze(3).to_broadcast([P, width // 4, PACK, 4]),
                 op=ALU.mult,
             )
 
-        w_codes, w_scales = {}, {}
-
-        def quantize_w(u):
-            w_codes[u] = work.tile([P, QC], U32, name="w_codes", align_bytes=64, bufs=8)
-            w_scales[u] = work.tile([P, QC], U8, name="w_scales", align_bytes=64, bufs=8)
-            quantize(w_codes[u][:], w_scales[u][:], w_bf[u][:].rearrange("p q r -> p (q r)"))
+        def quantize_w(first, end):
+            cols = slice(QC * first, QC * end)
+            quantize(w_codes[:, cols], w_scales[:, cols], w_bf[:, cols, :].rearrange("p q r -> p (q r)"))
 
         def y_of(u):
-            return y_bank[(u // 2) % 4][:, 2 * (u // 8) + u % 2, :]
+            return y_bank[(u + 1) // 4 % 4][:, (u + 1) % 4, :]
 
         def values(u):
             nc.tensor.matmul_mx(
                 out=y_of(u),
-                lhsT=w_codes[u][:].bitcast(FP8X4),
-                lhsT_scale=w_scales[u][:],
+                lhsT=w_codes[:, QC * u : QC * (u + 1)].bitcast(FP8X4),
+                lhsT_scale=w_scales[:, QC * u : QC * (u + 1)],
                 rhs=v_codes[:].bitcast(FP8X4),
                 rhs_scale=v_scales[:],
                 start=True,
@@ -182,8 +203,11 @@ def tile_rows_a_sigmoid_kb_onorm_kernel(tc, qT, kT, t, v, kb, gn, out):
                             op1=ALU.mult,
                         )
                     if u == end - 1:
-                        c, g = divmod(first, H)
-                        dst = out[g : g + end - first, QC * c : QC * (c + 1), :].rearrange("h q e -> q h e")
+                        g, c = UNIT[first]
+                        if UNIT[u][0] == g:
+                            dst = out[g, QC * c : QC * (c + end - first), :].rearrange("(c q) e -> q c e", q=QC)
+                        else:
+                            dst = out[g : g + end - first, QC * c : QC * (c + 1), :].rearrange("h q e -> q h e")
                         nc.sync.dma_start(out=dst, in_=result[i][:])
 
         interleave(q_bf[0], q_raw[0])
@@ -198,35 +222,41 @@ def tile_rows_a_sigmoid_kb_onorm_kernel(tc, qT, kT, t, v, kb, gn, out):
         quantize_k(2)
         scores((0, 0), (1, 0))
         scores((0, 1), (1, 1))
+        interleave(q_bf[1], q_raw[1])
+        interleave(q_bf[2], q_raw[2])
+        quantize_q(1)
         scores((2, 0), (3, 0))
         scores((2, 1))
-        interleave(q_bf[1], q_raw[1])
-        interleave(v_bf, v_raw)
-        quantize_q(1)
-        quantize(v_codes[:], v_scales[:], v_bf[:].rearrange("p e r -> p (e r)"))
+        interleave(q_bf[3], q_raw[3])
+        quantize_q(2)
 
-        for n in range(UNITS + 1):
-            if n < UNITS:
-                sigmoid(n)
-                if n + H < UNITS:
-                    scores((n + H - 1, 1), (n + H, 0))
-                elif n + H == UNITS:
-                    scores((n + H - 1, 1))
-                weigh(n)
-            if n >= 1:
-                quantize_w(n - 1)
-            if n in (0, 4):
-                interleave(q_bf[2 + n // 4], q_raw[2 + n // 4])
-            if n in (1, 5):
-                quantize_q(2 + n // 4)
-            if n in (5, 9):
-                for u in range(n - 5, n - 1):
+        weighed, quantized, multiplied = 0, 0, 0
+        for n in range(UNITS):
+            sigmoid(n)
+            if n + H < UNITS:
+                scores((n + H - 1, 1), (n + H, 0))
+            elif n + H == UNITS:
+                scores((n + H - 1, 1))
+            g, cs, rs = FILLS[n]
+            if rs[-1] == PACK - 1:
+                pieces = [len(cs)] if n < UNITS - 1 else [1] * len(cs)
+                for piece in pieces:
+                    weigh(weighed, weighed + piece)
+                    if n == 0:
+                        quantize_q(3)
+                    if quantized < weighed:
+                        quantize_w(quantized, weighed)
+                        quantized = weighed
+                    weighed += piece
+            if n == 4:
+                interleave(v_bf, v_raw)
+                quantize_w(quantized, weighed)
+                quantized = weighed
+                quantize(v_codes[:], v_scales[:], v_bf[:].rearrange("p e r -> p (e r)"))
+            if n >= UNITS - H:
+                for u in range(multiplied, quantized):
                     values(u)
-            if n == 12:
-                for u in range(8, 12):
-                    values(u)
-            if n > 12:
-                values(n - 1)
+                multiplied = quantized
 
         for b, (lo, hi) in enumerate(BATCHES):
             for u in range(lo, hi):
@@ -234,6 +264,11 @@ def tile_rows_a_sigmoid_kb_onorm_kernel(tc, qT, kT, t, v, kb, gn, out):
                 if u == lo and b >= 2:
                     root(b - 1)
                     finish(b - 1)
-            if b in (0, len(BATCHES) - 1):
+            if b == 0:
+                root(b)
+                finish(b)
+                quantize_w(UNITS - 1, UNITS)
+                values(UNITS - 1)
+            if b == len(BATCHES) - 1:
                 root(b)
                 finish(b)

@@ -76,9 +76,10 @@ def tile_rows_a_sigmoid_kb_onorm_kernel(tc, qT, kT, t, v, kb, gn, out):
             nc.sync.dma_start(out=q_raw[c][:], in_=q_hbm[:, :, QC * c : QC * (c + 1)])
 
         nc.vector.memset(zero[:], 0.0)
-        load_q(0)
+        nc.sync.dma_start(out=q_raw[0][: P // 2], in_=q_hbm[: P // 2, :, :QC])
+        nc.scalar.dma_start(out=q_raw[0][P // 2 :], in_=q_hbm[P // 2 :, :, :QC])
         for a in range(2):
-            for g in (2, 0, 3, 1):
+            for g in (0, 2, 1, 3):
                 queue = nc.sync if g < 2 else nc.scalar
                 queue.dma_start(
                     out=k_raw[a][ROWS * g : ROWS * (g + 1), :, :], in_=k_hbm[:, :, HALF * a : HALF * (a + 1)]
@@ -94,7 +95,7 @@ def tile_rows_a_sigmoid_kb_onorm_kernel(tc, qT, kT, t, v, kb, gn, out):
 
         def interleave(dst, src):
             nc.vector.tensor_copy(
-                out=dst[:].rearrange("p (a i) j -> p a j i", i=4), in_=src[:].rearrange("p j (a i) -> p a j i", i=4)
+                out=dst[:].rearrange("p (a i) j -> p a j i", i=2), in_=src[:].rearrange("p j (a i) -> p a j i", i=2)
             )
 
         def quantize(codes, scales, src):
@@ -155,9 +156,9 @@ def tile_rows_a_sigmoid_kb_onorm_kernel(tc, qT, kT, t, v, kb, gn, out):
             lo = QC * cs.index(c)
             width = QC * (end - first)
             nc.vector.tensor_tensor(
-                out=w_bf[:, QC * first : QC * end, :].rearrange("p (a i) r -> p a r i", i=4),
-                in0=prob[g, cs][:, :, lo : lo + width].rearrange("p r (a i) -> p a r i", i=4),
-                in1=t_sb[:].unsqueeze(1).unsqueeze(3).to_broadcast([P, width // 4, PACK, 4]),
+                out=w_bf[:, QC * first : QC * end, :].rearrange("p (a i) r -> p a r i", i=2),
+                in0=prob[g, cs][:, :, lo : lo + width].rearrange("p r (a i) -> p a r i", i=2),
+                in1=t_sb[:].unsqueeze(1).unsqueeze(3).to_broadcast([P, width // 2, PACK, 2]),
                 op=ALU.mult,
             )
 

@@ -9,6 +9,7 @@ F32 = mybir.dt.float32
 BF16 = mybir.dt.bfloat16
 U32 = mybir.dt.uint32
 U8 = mybir.dt.uint8
+I32 = mybir.dt.int32
 FP8X4 = mybir.dt.float8_e4m3fn_x4
 ACT = mybir.ActivationFunctionType
 ALU = mybir.AluOpType
@@ -16,12 +17,13 @@ ALU = mybir.AluOpType
 P = 128
 PACK = 4
 ROWS = 32
+K_ROWS = 3 * ROWS
 QC = 128
 CHUNKS = NQ // QC
 UNITS = CHUNKS * H
 HALF = N // 2
 S_HALF = HALF // PACK
-S_SPLIT = 40
+S_SPLIT = 44
 EPS = 256.0 * 1e-5
 ALL = (0, 1, 2, 3)
 PLAN = (
@@ -30,11 +32,13 @@ PLAN = (
     (((0,), ALL), ((1,), ALL), ((2, 3), (0, 1)), ((2, 3), (2, 3))),
     (((0, 1), (0, 1)), ((0, 1), (2, 3)), ((2, 3), (0, 1)), ((2, 3), (2, 3))),
 )
-FILLS = tuple((n % H,) + PLAN[n % H][n // H] for n in range(UNITS))
+HEADS = (0, 2, 0, 1, 3, 2, 1, 3, 0, 2, 1, 3, 0, 2, 1, 3)
+FILLS = tuple((g,) + PLAN[g][HEADS[:n].count(g)] for n, g in enumerate(HEADS))
+FREED = tuple(max([m for m in range(n) if HEADS[m] == g], default=0) for n, g in enumerate(HEADS))
 GROUPS = tuple((g, cs) for g, cs, rs in FILLS if rs[-1] == PACK - 1)
 UNIT = tuple((g, c) for g, cs in GROUPS for c in cs)
-BATCHES = ((0, 3), (3, 7), (7, 11), (11, 16))
-STORES = ((0, 3), (3, 4), (4, 5), (5, 7), (7, 9), (9, 11), (11, 12), (12, 14), (14, 15), (15, 16))
+BATCHES = ((0, 2), (2, 6), (6, 10), (10, 14), (14, 16))
+STORES = ((0, 1), (1, 2), (2, 3), (3, 4), (4, 5), (5, 7), (7, 9), (9, 11), (11, 13), (13, 14), (14, 15), (15, 16))
 
 
 def tile_rows_a_sigmoid_kb_onorm_kernel(tc, qT, kT, t, v, kb, gn, out):
@@ -52,10 +56,11 @@ def tile_rows_a_sigmoid_kb_onorm_kernel(tc, qT, kT, t, v, kb, gn, out):
         q_bf = [keep.tile([P, QC, PACK], BF16, name="q_bf%d" % c, align_bytes=64) for c in range(CHUNKS)]
         q_codes = [keep.tile([P, QC], U32, name="q_codes%d" % c, align_bytes=64) for c in range(CHUNKS)]
         q_scales = [keep.tile([P, QC], U8, name="q_scales%d" % c, align_bytes=64) for c in range(CHUNKS)]
-        k_raw = [keep.tile([P, PACK, HALF], F32, name="k_raw%d" % a) for a in range(2)]
+        k_raw = keep.tile([P, 2, PACK, HALF], F32)
         k_bf = keep.tile([P, PACK, P, PACK], BF16, align_bytes=64)
-        k_codes = keep.tile([P, N], U32, align_bytes=64)
-        k_scales = keep.tile([P, N], U8, align_bytes=64)
+        k_mx = keep.tile([P, (PACK + 1) * N], U8, align_bytes=64)
+        k_codes = k_mx[:, : PACK * N].bitcast(U32)
+        k_scales = k_mx[:, PACK * N :]
         v_raw = keep.tile([P, PACK, E], F32)
         v_bf = keep.tile([P, E, PACK], BF16, align_bytes=64)
         v_codes = keep.tile([P, E], U32, align_bytes=64)
@@ -76,22 +81,21 @@ def tile_rows_a_sigmoid_kb_onorm_kernel(tc, qT, kT, t, v, kb, gn, out):
             nc.sync.dma_start(out=q_raw[c][:], in_=q_hbm[:, :, QC * c : QC * (c + 1)])
 
         nc.vector.memset(zero[:], 0.0)
+        nc.vector.memset(k_scales.bitcast(U32), 0)
+        nc.vector.memset(k_raw[ROWS : 2 * ROWS].rearrange("p a j i -> p (a j i)").bitcast(U32), 0)
         nc.sync.dma_start(out=q_raw[0][: P // 2], in_=q_hbm[: P // 2, :, :QC])
         nc.scalar.dma_start(out=q_raw[0][P // 2 :], in_=q_hbm[P // 2 :, :, :QC])
         for a in range(2):
-            for g in (0, 2, 1, 3):
-                queue = nc.sync if g < 2 else nc.scalar
+            for g, queue in ((0, nc.sync), (2, nc.scalar)):
                 queue.dma_start(
-                    out=k_raw[a][ROWS * g : ROWS * (g + 1), :, :], in_=k_hbm[:, :, HALF * a : HALF * (a + 1)]
+                    out=k_raw[ROWS * g : ROWS * (g + 1), a, :, :], in_=k_hbm[:, :, HALF * a : HALF * (a + 1)]
                 )
+        nc.scalar.dma_start(out=kb_sb[:], in_=kb.rearrange("(p r) o -> p (r o)", r=PACK))
         nc.scalar.activation(out=warm[:], in_=zero[:], func=ACT.Sigmoid)
-        nc.sync.dma_start(out=kb_sb[:], in_=kb.rearrange("(p r) o -> p (r o)", r=PACK))
         load_q(1)
         nc.sync.dma_start(out=t_sb[:], in_=t.rearrange("(p r) o -> p (r o)", r=PACK))
         load_q(2)
         load_q(3)
-        nc.sync.dma_start(out=v_raw[:], in_=v.rearrange("o (p r) e -> (o p) r e", r=PACK))
-        nc.sync.dma_start(out=gn_sb[:], in_=gn)
 
         def interleave(dst, src):
             nc.vector.tensor_copy(
@@ -105,13 +109,15 @@ def tile_rows_a_sigmoid_kb_onorm_kernel(tc, qT, kT, t, v, kb, gn, out):
             quantize(q_codes[c][:], q_scales[c][:], q_bf[c][:].rearrange("p q j -> p (q j)"))
 
         def deal_k(a, lo, hi):
-            dst = k_bf[:, :, S_HALF * a + lo : S_HALF * a + hi, :].rearrange("p r s j -> p s r j")
-            src = k_raw[a][:, :, PACK * lo : PACK * hi].rearrange("p j (s r) -> p s r j", r=PACK)
+            dst = k_bf[:K_ROWS, :, S_HALF * a + lo : S_HALF * a + hi, :].rearrange("p r s j -> p s r j")
+            src = k_raw[:K_ROWS, a, :, PACK * lo : PACK * hi].rearrange("p j (s r) -> p s r j", r=PACK)
             return dst, src
 
-        def quantize_k(r0):
-            cols = slice(P * r0, P * (r0 + 2))
-            quantize(k_codes[:, cols], k_scales[:, cols], k_bf[:, r0 : r0 + 2, :, :].rearrange("p r s j -> p (r s j)"))
+        def quantize_k():
+            for r in range(PACK):
+                cols = slice(P * r, P * (r + 1))
+                src = k_bf[:K_ROWS, r, :, :].rearrange("p s j -> p (s j)")
+                quantize(k_codes[:K_ROWS, cols], k_scales[:K_ROWS, cols], src)
 
         def scores(*jobs):
             for step in range(2):
@@ -167,7 +173,7 @@ def tile_rows_a_sigmoid_kb_onorm_kernel(tc, qT, kT, t, v, kb, gn, out):
             quantize(w_codes[:, cols], w_scales[:, cols], w_bf[:, cols, :].rearrange("p q r -> p (q r)"))
 
         def y_of(u):
-            return y_bank[(u + 1) // 4 % 4][:, (u + 1) % 4, :]
+            return y_bank[(u + 2) // 4 % 4][:, (u + 2) % 4, :]
 
         def values(u):
             nc.tensor.matmul_mx(
@@ -212,44 +218,49 @@ def tile_rows_a_sigmoid_kb_onorm_kernel(tc, qT, kT, t, v, kb, gn, out):
                         nc.sync.dma_start(out=dst, in_=result[i][:])
 
         interleave(q_bf[0], q_raw[0])
-        dst, src = deal_k(0, 0, S_HALF)
-        nc.vector.tensor_copy(out=dst, in_=src)
-        quantize_q(0)
-        dst, src = deal_k(1, 0, S_SPLIT)
-        nc.vector.tensor_copy(out=dst, in_=src)
-        dst, src = deal_k(1, S_SPLIT, S_HALF)
-        nc.scalar.copy(out=dst, in_=src)
-        quantize_k(0)
-        quantize_k(2)
-        scores((0, 0), (1, 0))
-        scores((0, 1), (1, 1))
+        for a in range(2):
+            dst, src = deal_k(a, 0, S_SPLIT)
+            nc.vector.tensor_copy(out=dst, in_=src)
+            dst, src = deal_k(a, S_SPLIT, S_HALF)
+            nc.scalar.copy(out=dst, in_=src)
+            if a == 0:
+                quantize_q(0)
+        quantize_k()
+        for g in (0, 2):
+            nc.scalar.dma_start(
+                out=k_mx[ROWS * (g + 1) : ROWS * (g + 2), :].bitcast(I32),
+                in_=k_mx[ROWS * g : ROWS * (g + 1), :].bitcast(I32),
+            )
+        nc.scalar.dma_start(out=v_raw[:], in_=v.rearrange("o (p r) e -> (o p) r e", r=PACK))
+        nc.scalar.dma_start(out=gn_sb[:], in_=gn)
+        for n in range(2):
+            scores((n, 0))
+            scores((n, 1))
         interleave(q_bf[1], q_raw[1])
         interleave(q_bf[2], q_raw[2])
         quantize_q(1)
-        scores((2, 0), (3, 0))
-        scores((2, 1))
         interleave(q_bf[3], q_raw[3])
         quantize_q(2)
 
         weighed, quantized, multiplied = 0, 0, 0
         for n in range(UNITS):
             sigmoid(n)
-            if n + H < UNITS:
-                scores((n + H - 1, 1), (n + H, 0))
-            elif n + H == UNITS:
-                scores((n + H - 1, 1))
+            jobs = [(m, half) for m in range(2, UNITS) for half in range(2) if max(FREED[m], m - H + half) == n]
+            whole = [m for m, half in jobs if half == 1 and (m, 0) in jobs]
+            for m in whole:
+                scores((m, 0))
+                scores((m, 1))
+            scores(*[job for job in jobs if job[0] not in whole])
             g, cs, rs = FILLS[n]
             if rs[-1] == PACK - 1:
-                pieces = [len(cs)] if n < UNITS - 1 else [1] * len(cs)
-                for piece in pieces:
-                    weigh(weighed, weighed + piece)
-                    if n == 0:
-                        quantize_q(3)
-                    if quantized < weighed:
-                        quantize_w(quantized, weighed)
-                        quantized = weighed
-                    weighed += piece
-            if n == 4:
+                weigh(weighed, weighed + len(cs))
+                if n == 0:
+                    quantize_q(3)
+                if quantized < weighed:
+                    quantize_w(quantized, weighed)
+                    quantized = weighed
+                weighed += len(cs)
+            if n == 3:
                 interleave(v_bf, v_raw)
                 quantize_w(quantized, weighed)
                 quantized = weighed
@@ -268,8 +279,9 @@ def tile_rows_a_sigmoid_kb_onorm_kernel(tc, qT, kT, t, v, kb, gn, out):
             if b == 0:
                 root(b)
                 finish(b)
-                quantize_w(UNITS - 1, UNITS)
-                values(UNITS - 1)
+                quantize_w(quantized, UNITS)
+                for u in range(quantized, UNITS):
+                    values(u)
             if b == len(BATCHES) - 1:
                 root(b)
                 finish(b)

from contextlib import ExitStack

import concourse.mybir as mybir

H, D, NQ, N, E = 4, 128, 512, 512, 128
FLOPS = 2 * H * N * NQ * (D + E)

F32 = mybir.dt.float32
BF16 = mybir.dt.bfloat16
U32 = mybir.dt.uint32
U8 = mybir.dt.uint8
I32 = mybir.dt.int32
FP8X4 = mybir.dt.float8_e4m3fn_x4
ACT = mybir.ActivationFunctionType
ALU = mybir.AluOpType

P = 128
PACK = 4
ROWS = 32
K_ROWS = 3 * ROWS
QC = 128
CHUNKS = NQ // QC
UNITS = CHUNKS * H
HALF = N // 2
S_HALF = HALF // PACK
S_SPLIT = 44
EPS = 256.0 * 1e-5
ALL = (0, 1, 2, 3)
PLAN = (
    (((0,), ALL), ((1,), ALL), ((2, 3), (0, 1)), ((2, 3), (2, 3))),
    (((0,), ALL), ((1, 2), (0, 1)), ((1, 2), (2, 3)), ((3,), ALL)),
    (((0,), ALL), ((1,), ALL), ((2, 3), (0, 1)), ((2, 3), (2, 3))),
    (((0, 1), (0, 1)), ((0, 1), (2, 3)), ((2, 3), (0, 1)), ((2, 3), (2, 3))),
)
HEADS = (0, 2, 0, 1, 3, 2, 1, 3, 0, 2, 1, 3, 0, 2, 1, 3)
FILLS = tuple((g,) + PLAN[g][HEADS[:n].count(g)] for n, g in enumerate(HEADS))
FREED = tuple(max([m for m in range(n) if HEADS[m] == g], default=0) for n, g in enumerate(HEADS))
GROUPS = tuple((g, cs) for g, cs, rs in FILLS if rs[-1] == PACK - 1)
UNIT = tuple((g, c) for g, cs in GROUPS for c in cs)
BATCHES = ((0, 2), (2, 6), (6, 10), (10, 14), (14, 16))
STORES = ((0, 1), (1, 2), (2, 3), (3, 4), (4, 5), (5, 7), (7, 9), (9, 11), (11, 13), (13, 14), (14, 15), (15, 16))


def tile_rows_a_sigmoid_kb_onorm_kernel(tc, qT, kT, t, v, kb, gn, out):
    nc = tc.nc
    with ExitStack() as ctx:
        keep = ctx.enter_context(tc.tile_pool(name="keep", bufs=1))
        work = ctx.enter_context(tc.tile_pool(name="work", bufs=4))
        psum = ctx.enter_context(tc.psum_pool(name="psum", bufs=1))
        ctx.enter_context(tc.manual_schedule())

        s_bank = [psum.tile([P, PACK * QC], F32, name="s_bank%d" % g) for g in range(H)]
        y_bank = [psum.tile([P, PACK, E], F32, name="y_bank%d" % b) for b in range(4)]

        q_raw = [keep.tile([P, PACK, QC], F32, name="q_raw%d" % c) for c in range(CHUNKS)]
        q_bf = [keep.tile([P, QC, PACK], BF16, name="q_bf%d" % c, align_bytes=64) for c in range(CHUNKS)]
        q_codes = [keep.tile([P, QC], U32, name="q_codes%d" % c, align_bytes=64) for c in range(CHUNKS)]
        q_scales = [keep.tile([P, QC], U8, name="q_scales%d" % c, align_bytes=64) for c in range(CHUNKS)]
        k_raw = keep.tile([P, 2, PACK, HALF], F32)
        k_bf = keep.tile([P, PACK, P, PACK], BF16, align_bytes=64)
        k_mx = keep.tile([P, (PACK + 1) * N], U8, align_bytes=64)
        k_codes = k_mx[:, : PACK * N].bitcast(U32)
        k_scales = k_mx[:, PACK * N :]
        v_raw = keep.tile([P, PACK, E], F32)
        v_bf = keep.tile([P, E, PACK], BF16, align_bytes=64)
        v_codes = keep.tile([P, E], U32, align_bytes=64)
        v_scales = keep.tile([P, E], U8, align_bytes=64)
        t_sb = keep.tile([P, PACK], F32)
        kb_sb = keep.tile([P, PACK], F32)
        gn_sb = keep.tile([P, E], F32)
        zero = keep.tile([P, 1], F32)
        warm = keep.tile([P, 1], F32)
        sumsq = keep.tile([P, UNITS], F32)
        rstd = [keep.tile([P, hi - lo], F32, name="rstd%d" % lo) for lo, hi in BATCHES]
        result = [keep.tile([P, hi - lo, E], F32, name="result%d" % lo) for lo, hi in STORES]

        q_hbm = qT.rearrange("h (p j) q -> (h p) j q", j=PACK)
        k_hbm = kT.rearrange("o (p j) i -> (o p) j i", j=PACK)

        def load_q(c):
            nc.sync.dma_start(out=q_raw[c][:], in_=q_hbm[:, :, QC * c : QC * (c + 1)])

        nc.vector.memset(zero[:], 0.0)
        nc.vector.memset(k_scales.bitcast(U32), 0)
        nc.vector.memset(k_raw[ROWS : 2 * ROWS].rearrange("p a j i -> p (a j i)").bitcast(U32), 0)
        nc.sync.dma_start(out=q_raw[0][: P // 2], in_=q_hbm[: P // 2, :, :QC])
        nc.scalar.dma_start(out=q_raw[0][P // 2 :], in_=q_hbm[P // 2 :, :, :QC])
        for a in range(2):
            for g, queue in ((0, nc.sync), (2, nc.scalar)):
                queue.dma_start(
                    out=k_raw[ROWS * g : ROWS * (g + 1), a, :, :], in_=k_hbm[:, :, HALF * a : HALF * (a + 1)]
                )
        nc.scalar.dma_start(out=kb_sb[:], in_=kb.rearrange("(p r) o -> p (r o)", r=PACK))
        nc.scalar.activation(out=warm[:], in_=zero[:], func=ACT.Sigmoid)
        load_q(1)
        nc.sync.dma_start(out=t_sb[:], in_=t.rearrange("(p r) o -> p (r o)", r=PACK))
        load_q(2)
        load_q(3)

        def interleave(dst, src):
            nc.vector.tensor_copy(
                out=dst[:].rearrange("p (a i) j -> p a j i", i=2), in_=src[:].rearrange("p j (a i) -> p a j i", i=2)
            )

        def quantize(codes, scales, src):
            nc.vector.quantize_mx(out=codes.bitcast(FP8X4), scales=scales, in_=src)

        def quantize_q(c):
            quantize(q_codes[c][:], q_scales[c][:], q_bf[c][:].rearrange("p q j -> p (q j)"))

        def deal_k(a, lo, hi):
            dst = k_bf[:K_ROWS, :, S_HALF * a + lo : S_HALF * a + hi, :].rearrange("p r s j -> p s r j")
            src = k_raw[:K_ROWS, a, :, PACK * lo : PACK * hi].rearrange("p j (s r) -> p s r j", r=PACK)
            return dst, src

        def quantize_k():
            for r in range(PACK):
                cols = slice(P * r, P * (r + 1))
                src = k_bf[:K_ROWS, r, :, :].rearrange("p s j -> p (s j)")
                quantize(k_codes[:K_ROWS, cols], k_scales[:K_ROWS, cols], src)

        def scores(*jobs):
            for step in range(2):
                for n, half in jobs:
                    g, cs, rs = FILLS[n]
                    place = 2 * half + step
                    r, c = rs[place // len(cs)], cs[place % len(cs)]
                    rows = slice(ROWS * g, ROWS * (g + 1))
                    cols = slice(P * r, P * (r + 1))
                    nc.tensor.matmul_mx(
                        out=s_bank[g][:, QC * place : QC * (place + 1)],
                        lhsT=k_codes[rows, cols].bitcast(FP8X4),
                        lhsT_scale=k_scales[rows, cols],
                        rhs=q_codes[c][rows, :].bitcast(FP8X4),
                        rhs_scale=q_scales[c][rows, :],
                        start=True,
                        stop=True,
                    )

        prob = {}
        for g, cs in GROUPS:
            prob[g, cs] = keep.tile([P, PACK, QC * len(cs)], F32, name="prob%d_%d" % (g, cs[0]))

        def sigmoid(n):
            g, cs, rs = FILLS[n]
            width = QC * len(cs)
            for i, r in enumerate(rs):
                nc.scalar.activation(
                    out=prob[g, cs][:, r, :],
                    in_=s_bank[g][:, width * i : width * (i + 1)],
                    func=ACT.Sigmoid,
                    bias=kb_sb[:, r : r + 1],
                )

        w_bf = keep.tile([P, UNITS * QC, PACK], BF16, align_bytes=64)
        w_codes = keep.tile([P, UNITS * QC], U32, align_bytes=64)
        w_scales = keep.tile([P, UNITS * QC], U8, align_bytes=64)

        def weigh(first, end):
            g, c = UNIT[first]
            cs = [chunks for head, chunks in GROUPS if head == g and c in chunks][0]
            lo = QC * cs.index(c)
            width = QC * (end - first)
            nc.vector.tensor_tensor(
                out=w_bf[:, QC * first : QC * end, :].rearrange("p (a i) r -> p a r i", i=2),
                in0=prob[g, cs][:, :, lo : lo + width].rearrange("p r (a i) -> p a r i", i=2),
                in1=t_sb[:].unsqueeze(1).unsqueeze(3).to_broadcast([P, width // 2, PACK, 2]),
                op=ALU.mult,
            )

        def quantize_w(first, end):
            cols = slice(QC * first, QC * end)
            quantize(w_codes[:, cols], w_scales[:, cols], w_bf[:, cols, :].rearrange("p q r -> p (q r)"))

        def y_of(u):
            return y_bank[(u + 2) // 4 % 4][:, (u + 2) % 4, :]

        def values(u):
            nc.tensor.matmul_mx(
                out=y_of(u),
                lhsT=w_codes[:, QC * u : QC * (u + 1)].bitcast(FP8X4),
                lhsT_scale=w_scales[:, QC * u : QC * (u + 1)],
                rhs=v_codes[:].bitcast(FP8X4),
                rhs_scale=v_scales[:],
                start=True,
                stop=True,
            )

        def square(u):
            squares = work.tile([P, E], BF16, name="squares")
            nc.scalar.activation(out=squares[:], in_=y_of(u), func=ACT.Square, accum_out=sumsq[:, u : u + 1])

        def root(b):
            lo, hi = BATCHES[b]
            nc.scalar.activation(
                out=rstd[b][:], in_=sumsq[:, lo:hi], func=ACT.Abs_reciprocal_sqrt, scale=1.0 / E, bias=EPS
            )

        def finish(b):
            lo, hi = BATCHES[b]
            for u in range(lo, hi):
                for i, (first, end) in enumerate(STORES):
                    if first <= u < end:
                        nc.vector.scalar_tensor_tensor(
                            out=result[i][:, u - first, :],
                            in0=y_of(u),
                            scalar=rstd[b][:, u - lo : u - lo + 1],
                            in1=gn_sb[:],
                            op0=ALU.mult,
                            op1=ALU.mult,
                        )
                    if u == end - 1:
                        g, c = UNIT[first]
                        if UNIT[u][0] == g:
                            dst = out[g, QC * c : QC * (c + end - first), :].rearrange("(c q) e -> q c e", q=QC)
                        else:
                            dst = out[g : g + end - first, QC * c : QC * (c + 1), :].rearrange("h q e -> q h e")
                        nc.sync.dma_start(out=dst, in_=result[i][:])

        interleave(q_bf[0], q_raw[0])
        for a in range(2):
            dst, src = deal_k(a, 0, S_SPLIT)
            nc.vector.tensor_copy(out=dst, in_=src)
            dst, src = deal_k(a, S_SPLIT, S_HALF)
            nc.scalar.copy(out=dst, in_=src)
            if a == 0:
                quantize_q(0)
        quantize_k()
        for g in (0, 2):
            nc.scalar.dma_start(
                out=k_mx[ROWS * (g + 1) : ROWS * (g + 2), :].bitcast(I32),
                in_=k_mx[ROWS * g : ROWS * (g + 1), :].bitcast(I32),
            )
        nc.scalar.dma_start(out=v_raw[:], in_=v.rearrange("o (p r) e -> (o p) r e", r=PACK))
        nc.scalar.dma_start(out=gn_sb[:], in_=gn)
        for n in range(2):
            scores((n, 0))
            scores((n, 1))
        interleave(q_bf[1], q_raw[1])
        interleave(q_bf[2], q_raw[2])
        quantize_q(1)
        interleave(q_bf[3], q_raw[3])
        quantize_q(2)

        weighed, quantized, multiplied = 0, 0, 0
        for n in range(UNITS):
            sigmoid(n)
            jobs = [(m, half) for m in range(2, UNITS) for half in range(2) if max(FREED[m], m - H + half) == n]
            whole = [m for m, half in jobs if half == 1 and (m, 0) in jobs]
            for m in whole:
                scores((m, 0))
                scores((m, 1))
            scores(*[job for job in jobs if job[0] not in whole])
            g, cs, rs = FILLS[n]
            if rs[-1] == PACK - 1:
                weigh(weighed, weighed + len(cs))
                if n == 0:
                    quantize_q(3)
                if quantized < weighed:
                    quantize_w(quantized, weighed)
                    quantized = weighed
                weighed += len(cs)
            if n == 3:
                interleave(v_bf, v_raw)
                quantize_w(quantized, weighed)
                quantized = weighed
                quantize(v_codes[:], v_scales[:], v_bf[:].rearrange("p e r -> p (e r)"))
            if n >= UNITS - H:
                for u in range(multiplied, quantized):
                    values(u)
                multiplied = quantized

        for b, (lo, hi) in enumerate(BATCHES):
            for u in range(lo, hi):
                square(u)
                if u == lo and b >= 2:
                    root(b - 1)
                    finish(b - 1)
            if b == 0:
                root(b)
                finish(b)
                quantize_w(quantized, UNITS)
                for u in range(quantized, UNITS):
                    values(u)
            if b == len(BATCHES) - 1:
                root(b)
                finish(b)
